import numpy as np
import ml_dtypes


def mxq(x, axis, fmt="e4m3"):
    dtype, down = {"e4m3": (ml_dtypes.float8_e4m3fn, 7), "e5m2": (ml_dtypes.float8_e5m2, 14)}[fmt]
    v = np.moveaxis(np.asarray(x, np.float32).astype(ml_dtypes.bfloat16).astype(np.float64), axis, -1)
    blocks = v.reshape(v.shape[:-1] + (-1, 32))
    amax = np.abs(blocks).max(-1, keepdims=True)
    byte = np.maximum(np.where(amax > 0, np.frexp(amax)[1] - 1 + 127, 0) - down, 1)
    scale = np.exp2(byte - 127.0)
    codes = (blocks / scale).astype(np.float32).astype(dtype).astype(np.float64)
    return np.moveaxis((codes * scale).reshape(v.shape), -1, axis)


WIDE = False


def mx_kscale(k):
    if not WIDE:
        return np.ones(k)
    levels = np.array([10, -10, 5, -5, 0])
    if k % 512:
        return np.exp2(np.random.permutation(np.resize(levels, k // 32))).repeat(32)
    a = np.empty((k // 512, 16))
    for p in range(k // 512):
        a[p, :8] = np.random.permutation(np.resize(levels, 8))
        for g in range(8):
            far = levels[np.abs(levels - a[p, g]) >= 10]
            a[p, g + 8] = far[np.random.randint(len(far))]
    return np.exp2(a.ravel()).repeat(32)


def f64(x):
    return np.asarray(x).astype(np.float64)


def striped(idx):
    return np.tile(idx.reshape(-1, 16).T, (8, 1)).astype(np.uint16)


def unstriped(offs):
    return offs[:16].T.reshape(-1).astype(np.int64)


def pack_weight(w):
    k, n = w.shape
    w = f64(np.asarray(w, np.float32).astype(ml_dtypes.bfloat16)).reshape(k // 32, 32, n)
    amax = np.abs(w).max(1)
    byte = np.clip(np.where(amax > 0, np.frexp(amax)[1] - 1 + 127 - 7, 1), 1, 254)
    scaled = (w * np.exp2(127.0 - byte)[:, None, :]).reshape(k, n).astype(np.float32)
    words = np.ascontiguousarray(scaled.reshape(k // 512, 128, 4, n).transpose(0, 1, 3, 2)).astype(ml_dtypes.float8_e4m3fn).view(np.uint8)
    return words, np.ascontiguousarray(byte.astype(np.uint8).reshape(k // 512, 16, n))


def unpack_weight(words, scales):
    g, p, n, _ = words.shape
    vals = np.ascontiguousarray(words).view(ml_dtypes.float8_e4m3fn).astype(np.float64) * np.repeat(np.exp2(scales.astype(np.float64) - 127.0), 8, axis=1)[..., None]
    return vals.transpose(0, 1, 3, 2).reshape(g * 512, n)


K, T, N, U = 512, 512, 256, 1024
P = 2 ** 7


def setup_inputs():
    n = np.random.standard_normal
    s = mx_kscale(K)[:, None]
    packed_xT = pack_weight(n((K, T)) * s)
    return {
        "x_words": packed_xT[0],
        "x_scales": packed_xT[1],
        "mem": n((N, U)).astype(np.float32),
        "w1": (n((K, N)) / np.sqrt(K) / s).astype(np.float32),
        "old": np.tile(np.random.uniform(0.5, 0.95, T), (P, 1)).astype(np.float32),
        "new": np.tile(np.random.uniform(0.05, 0.5, T), (P, 1)).astype(np.float32),
        "slot": striped(np.random.permutation(U)[:T]),
    }


def reference(x_words, x_scales, mem, w1, old, new, slot):
    xq = unpack_weight(x_words, x_scales)
    y = mxq(f64(w1), 0, "e4m3").T @ xq
    out = f64(mem).copy()
    out[:, unstriped(slot)] = f64(mem)[:, unstriped(slot)] * f64(old)[:1] + y * f64(new)[:1]
    return out

@@ -1,0 +1,95 @@
+from contextlib import ExitStack
+
+import concourse.mybir as mybir
+from concourse.masks import make_identity
+
+K, T, N, U = 512, 512, 256, 1024
+FLOPS = 2 * K * T * N
+P = 128
+PACK = 4
+
+F32 = mybir.dt.float32
+BF16 = mybir.dt.bfloat16
+I32 = mybir.dt.int32
+U32 = mybir.dt.uint32
+U16 = mybir.dt.uint16
+U8 = mybir.dt.uint8
+FP8X4 = mybir.dt.float8_e4m3fn_x4
+MULT = mybir.AluOpType.mult
+ADD = mybir.AluOpType.add
+COPY = mybir.ActivationFunctionType.Copy
+
+
+def tile_picked_wema_none_l_kernel(tc, x_words, x_scales, mem, w1, old, new, slot, out):
+    nc = tc.nc
+    with ExitStack() as ctx:
+        sb = ctx.enter_context(tc.tile_pool(name="sb", bufs=1))
+        ps = ctx.enter_context(tc.psum_pool(name="ps", bufs=1))
+
+        offs = sb.tile([P, T // 16], U16, name="offs")
+        mems = [sb.tile([P, U], F32, name=f"mem{b}") for b in range(2)]
+        w_raw = sb.tile([P, PACK, N], F32, name="w_raw")
+        xw = sb.tile([P, T], U32, name="xw", align_bytes=64)
+        xs = sb.tile([P, T], U8, name="xs", align_bytes=64)
+        old_col = sb.tile([P, 4], F32, name="old_col")
+        new_rows = sb.tile([P, P], F32, name="new_rows")
+        ident = sb.tile([P, P], F32, name="ident")
+
+        nc.gpsimd.memset(xs[:].bitcast(I32), 0)
+        make_identity(nc, ident[:])
+
+        nc.sync.dma_start(old_col[:], old[0, :].rearrange("(p b) -> p b", b=4))
+        nc.sync.dma_start(new_rows[:], new[0:32, :].rearrange("r (c n) -> (r c) n", n=P))
+        nc.sync.dma_start(w_raw[:], w1.rearrange("(p j) n -> p j n", j=PACK))
+        nc.sync.dma_start(xw[:].bitcast(I32), x_words[0].rearrange("p n t -> p (n t)").bitcast(I32))
+        for q in range(4):
+            nc.sync.dma_start(xs[32 * q : 32 * q + 4, :].bitcast(I32), x_scales[0, 4 * q : 4 * q + 4, :].bitcast(I32))
+        nc.sync.dma_start(mems[0][:], mem[0:P, :])
+        nc.sync.dma_start(offs[:], slot)
+        nc.sync.dma_start(mems[1][:], mem[P : 2 * P, :])
+
+        old_ps = ps.tile([P, 4, P], F32, name="old_ps", tag="bank0")
+        for b in range(4):
+            nc.tensor.transpose(old_ps[:, b, :], old_col[:, b : b + 1].to_broadcast([P, P]), ident[:])
+        old_sb = sb.tile([P, T], F32, name="old_sb")
+        nc.scalar.copy(old_sb[:].rearrange("p (n b) -> p n b", b=4), old_ps[:].rearrange("p b n -> p n b"))
+        new_ps = ps.tile([P, P], F32, name="new_ps", tag="bank1")
+        nc.tensor.transpose(new_ps[:], new_rows[:], ident[:])
+        new_col = sb.tile([P, 4], F32, name="new_col")
+        nc.scalar.copy(new_col[:], new_ps[:, 0:4])
+
+        grouped = [sb.tile([P, P, PACK], BF16, name=f"grouped{b}", align_bytes=64) for b in range(2)]
+        wq = [sb.tile([P, P], U32, name=f"wq{b}", align_bytes=64) for b in range(2)]
+        ws = [sb.tile([P, P], U8, name=f"ws{b}", align_bytes=64) for b in range(2)]
+        for b in range(2):
+            nc.vector.tensor_copy(
+                grouped[b][:].rearrange("p (c i) t -> p c t i", i=4),
+                w_raw[:, :, b * P : (b + 1) * P].rearrange("p t (c i) -> p c t i", i=4),
+            )
+        for b in range(2):
+            nc.vector.quantize_mx(out=wq[b][:].bitcast(FP8X4), scales=ws[b][:], in_=grouped[b][:].rearrange("p n t -> p (n t)"))
+
+        kept = [sb.tile([P, T], F32, name=f"kept{b}") for b in range(2)]
+        for b in range(2):
+            nc.vector.tensor_tensor(kept[b][:], mems[b][:].indirect(offs[:]), old_sb[:], MULT)
+
+        for b in range(2):
+            if b == 0:
+                halves = [ps.tile([P, 2, P], F32, name=f"yt0{h}", tag=f"bank{h}") for h in range(2)]
+                yt = [halves[c // 2][:, c % 2, :] for c in range(4)]
+            else:
+                whole = ps.tile([P, 4, P], F32, name="yt1", tag="bank2")
+                yt = [whole[:, c, :] for c in range(4)]
+            for c in range(4):
+                cols = slice(c * P, (c + 1) * P)
+                nc.tensor.matmul_mx(out=yt[c], lhsT=xw[:, cols].bitcast(FP8X4), lhsT_scale=xs[:, cols],
+                                    rhs=wq[b][:].bitcast(FP8X4), rhs_scale=ws[b][:], start=True, stop=True)
+            back = ps.tile([P, 4, P], F32, name=f"back{b}", tag=f"bank{2 + b}")
+            for c in range(4):
+                z = sb.tile([P, P], F32, name=f"z{b}{c}")
+                nc.scalar.activation(z[:], yt[c], COPY, scale=new_col[:, c : c + 1])
+                nc.tensor.transpose(back[:, c, :], z[:], ident[:])
+            fresh = sb.tile([P, T], F32, name=f"fresh{b}")
+            nc.scalar.copy(fresh[:], back[:].rearrange("p c n -> p (c n)"))
+            nc.vector.tensor_tensor(mems[b][:].indirect(offs[:]), kept[b][:], fresh[:], ADD)
+            nc.sync.dma_start(out[b * P : (b + 1) * P, :], mems[b][:])

@@ -39,11 +39,11 @@ def tile_picked_wema_none_l_kernel(tc, x_words, x_scales, mem, w1, old, new, slo
         make_identity(nc, ident[:])
 
         nc.sync.dma_start(old_col[:], old[0, :].rearrange("(p b) -> p b", b=4))
-        nc.sync.dma_start(new_rows[:], new[0:32, :].rearrange("r (c n) -> (r c) n", n=P))
         nc.sync.dma_start(w_raw[:], w1.rearrange("(p j) n -> p j n", j=PACK))
+        nc.sync.dma_start(new_rows[:], new[0:32, :].rearrange("r (c n) -> (r c) n", n=P))
         nc.sync.dma_start(xw[:].bitcast(I32), x_words[0].rearrange("p n t -> p (n t)").bitcast(I32))
         for q in range(4):
-            nc.sync.dma_start(xs[32 * q : 32 * q + 4, :].bitcast(I32), x_scales[0, 4 * q : 4 * q + 4, :].bitcast(I32))
+            nc.scalar.dma_start(xs[32 * q : 32 * q + 4, :].bitcast(I32), x_scales[0, 4 * q : 4 * q + 4, :].bitcast(I32))
         nc.sync.dma_start(mems[0][:], mem[0:P, :])
         nc.sync.dma_start(offs[:], slot)
         nc.sync.dma_start(mems[1][:], mem[P : 2 * P, :])
@@ -84,12 +84,13 @@ def tile_picked_wema_none_l_kernel(tc, x_words, x_scales, mem, w1, old, new, slo
                 cols = slice(c * P, (c + 1) * P)
                 nc.tensor.matmul_mx(out=yt[c], lhsT=xw[:, cols].bitcast(FP8X4), lhsT_scale=xs[:, cols],
                                     rhs=wq[b][:].bitcast(FP8X4), rhs_scale=ws[b][:], start=True, stop=True)
-            back = ps.tile([P, 4, P], F32, name=f"back{b}", tag=f"bank{2 + b}")
+            back = [ps.tile([P, 2, P], F32, name=f"back{b}{h}", tag=f"bank{2 + 2 * b + h}") for h in range(2)]
             for c in range(4):
                 z = sb.tile([P, P], F32, name=f"z{b}{c}")
                 nc.scalar.activation(z[:], yt[c], COPY, scale=new_col[:, c : c + 1])
-                nc.tensor.transpose(back[:, c, :], z[:], ident[:])
+                nc.tensor.transpose(back[c // 2][:, c % 2, :], z[:], ident[:])
             fresh = sb.tile([P, T], F32, name=f"fresh{b}")
-            nc.scalar.copy(fresh[:], back[:].rearrange("p c n -> p (c n)"))
+            for h in range(2):
+                nc.scalar.copy(fresh[:, h * 2 * P : (h + 1) * 2 * P], back[h][:].rearrange("p c n -> p (c n)"))
             nc.vector.tensor_tensor(mems[b][:].indirect(offs[:]), kept[b][:], fresh[:], ADD)
             nc.sync.dma_start(out[b * P : (b + 1) * P, :], mems[b][:])

@@ -1,12 +1,12 @@
 from contextlib import ExitStack
 
 import concourse.mybir as mybir
-from concourse.masks import make_identity
 
 K, T, N, U = 512, 512, 256, 1024
 FLOPS = 2 * K * T * N
 P = 128
 PACK = 4
+FIRST = 128
 
 F32 = mybir.dt.float32
 BF16 = mybir.dt.bfloat16
@@ -26,71 +26,82 @@ def tile_picked_wema_none_l_kernel(tc, x_words, x_scales, mem, w1, old, new, slo
         sb = ctx.enter_context(tc.tile_pool(name="sb", bufs=1))
         ps = ctx.enter_context(tc.psum_pool(name="ps", bufs=1))
 
+        pieces = [(0, FIRST), (FIRST, T)]
         offs = sb.tile([P, T // 16], U16, name="offs")
         mems = [sb.tile([P, U], F32, name=f"mem{b}") for b in range(2)]
         w_raw = sb.tile([P, PACK, N], F32, name="w_raw")
-        xw = sb.tile([P, T], U32, name="xw", align_bytes=64)
+        xw = [sb.tile([P, hi - lo], U32, name=f"xw{lo}", align_bytes=64) for lo, hi in pieces]
         xs = sb.tile([P, T], U8, name="xs", align_bytes=64)
         old_col = sb.tile([P, 4], F32, name="old_col")
-        new_rows = sb.tile([P, P], F32, name="new_rows")
+        new_rows = sb.tile([P, 32], F32, name="new_rows", align_bytes=64)
         ident = sb.tile([P, P], F32, name="ident")
+        words = x_words[0].rearrange("p n t -> p (n t)").bitcast(I32)
 
         nc.gpsimd.memset(xs[:].bitcast(I32), 0)
-        make_identity(nc, ident[:])
+        ones = sb.tile([P, 32], F32, name="ones")
+        ramp = sb.tile([P, 32], F32, name="ramp", align_bytes=64)
+        turned = sb.tile([P, 32], F32, name="turned", align_bytes=64)
+        nc.vector.memset(ones[:], 1.0)
+        nc.vector.memset(ident[:], 0.0)
+        nc.vector.tensor_tensor_scan(ramp[:], ones[:], ones[:], 0.0, MULT, ADD)
+        nc.vector.transpose(turned[:], ramp[:])
+        for q in range(4):
+            rows = slice(32 * q, 32 * q + 32)
+            nc.vector.tensor_tensor(ident[rows, rows], ramp[rows, :], turned[rows, :], mybir.AluOpType.is_equal)
 
         nc.sync.dma_start(old_col[:], old[0, :].rearrange("(p b) -> p b", b=4))
-        nc.sync.dma_start(w_raw[:], w1.rearrange("(p j) n -> p j n", j=PACK))
-        nc.sync.dma_start(new_rows[:], new[0:32, :].rearrange("r (c n) -> (r c) n", n=P))
-        nc.sync.dma_start(xw[:].bitcast(I32), x_words[0].rearrange("p n t -> p (n t)").bitcast(I32))
-        for q in range(4):
-            nc.scalar.dma_start(xs[32 * q : 32 * q + 4, :].bitcast(I32), x_scales[0, 4 * q : 4 * q + 4, :].bitcast(I32))
-        nc.sync.dma_start(mems[0][:], mem[0:P, :])
         nc.sync.dma_start(offs[:], slot)
+        nc.sync.dma_start(new_rows[:], new[0:8, :].rearrange("u (c q i) -> q (u c) i", c=4, q=4))
+        nc.sync.dma_start(w_raw[:], w1.rearrange("(p j) n -> p j n", j=PACK))
+        nc.sync.dma_start(xs[0:4, :].bitcast(I32), x_scales[0, 0:4, :].bitcast(I32))
+        nc.sync.dma_start(xs[32:36, :].bitcast(I32), x_scales[0, 4:8, :].bitcast(I32))
+        nc.sync.dma_start(xw[0][:].bitcast(I32), words[:, 0:FIRST])
+        nc.sync.dma_start(mems[0][:], mem[0:P, :])
+        nc.sync.dma_start(xs[64:68, :].bitcast(I32), x_scales[0, 8:12, :].bitcast(I32))
+        nc.sync.dma_start(xs[96:100, :].bitcast(I32), x_scales[0, 12:16, :].bitcast(I32))
         nc.sync.dma_start(mems[1][:], mem[P : 2 * P, :])
+        nc.sync.dma_start(xw[1][:].bitcast(I32), words[:, FIRST:T])
 
-        old_ps = ps.tile([P, 4, P], F32, name="old_ps", tag="bank0")
+        old_ps = ps.tile([P, 4, P], F32, name="old_ps", tag="product0")
         for b in range(4):
             nc.tensor.transpose(old_ps[:, b, :], old_col[:, b : b + 1].to_broadcast([P, P]), ident[:])
         old_sb = sb.tile([P, T], F32, name="old_sb")
         nc.scalar.copy(old_sb[:].rearrange("p (n b) -> p n b", b=4), old_ps[:].rearrange("p b n -> p n b"))
-        new_ps = ps.tile([P, P], F32, name="new_ps", tag="bank1")
-        nc.tensor.transpose(new_ps[:], new_rows[:], ident[:])
-        new_col = sb.tile([P, 4], F32, name="new_col")
-        nc.scalar.copy(new_col[:], new_ps[:, 0:4])
+        new_col = sb.tile([P, 32], F32, name="new_col", align_bytes=64)
+        nc.vector.transpose(new_col[:], new_rows[:])
 
         grouped = [sb.tile([P, P, PACK], BF16, name=f"grouped{b}", align_bytes=64) for b in range(2)]
-        wq = [sb.tile([P, P], U32, name=f"wq{b}", align_bytes=64) for b in range(2)]
-        ws = [sb.tile([P, P], U8, name=f"ws{b}", align_bytes=64) for b in range(2)]
+        wq = sb.tile([P, N], U32, name="wq", align_bytes=64)
+        ws = sb.tile([P, N], U8, name="ws", align_bytes=64)
         for b in range(2):
             nc.vector.tensor_copy(
                 grouped[b][:].rearrange("p (c i) t -> p c t i", i=4),
                 w_raw[:, :, b * P : (b + 1) * P].rearrange("p t (c i) -> p c t i", i=4),
             )
         for b in range(2):
-            nc.vector.quantize_mx(out=wq[b][:].bitcast(FP8X4), scales=ws[b][:], in_=grouped[b][:].rearrange("p n t -> p (n t)"))
+            rows = slice(b * P, (b + 1) * P)
+            nc.vector.quantize_mx(out=wq[:, rows].bitcast(FP8X4), scales=ws[:, rows], in_=grouped[b][:].rearrange("p n t -> p (n t)"))
 
         kept = [sb.tile([P, T], F32, name=f"kept{b}") for b in range(2)]
         for b in range(2):
             nc.vector.tensor_tensor(kept[b][:], mems[b][:].indirect(offs[:]), old_sb[:], MULT)
 
+        for lo, hi in [(0, P), (P, 2 * P), (2 * P, T)]:
+            chunks = (hi - lo) // P
+            backs = [ps.tile([P, chunks, P], F32, name=f"back{b}{lo}", tag=f"back{b}{lo // P % 2}") for b in range(2)]
+            for i in range(chunks):
+                c = lo // P + i
+                yt = ps.tile([P, N], F32, name=f"yt{c}", tag=f"product{c}")
+                nc.tensor.matmul_mx(out=yt[:], lhsT=(xw[0][:] if c == 0 else xw[1][:, (c - 1) * P : c * P]).bitcast(FP8X4), lhsT_scale=xs[:, c * P : (c + 1) * P],
+                                    rhs=wq[:].bitcast(FP8X4), rhs_scale=ws[:], start=True, stop=True)
+                z = sb.tile([P, N], F32, name=f"z{c}")
+                for cols in ([slice(0, P), slice(P, N)] if c == 0 else [slice(0, N)]):
+                    nc.scalar.activation(z[:, cols], yt[:, cols], COPY, scale=new_col[:, c : c + 1])
+                for b in range(2):
+                    nc.tensor.transpose(backs[b][:, i, :], z[:, b * P : (b + 1) * P], ident[:])
+            for b in range(2):
+                fresh = sb.tile([P, hi - lo], F32, name=f"fresh{b}{lo}")
+                nc.scalar.copy(fresh[:], backs[b][:].rearrange("p c n -> p (c n)"))
+                nc.vector.tensor_tensor(mems[b][:].indirect(offs[:, lo // 16 : hi // 16]), kept[b][:, lo:hi], fresh[:], ADD)
         for b in range(2):
-            if b == 0:
-                halves = [ps.tile([P, 2, P], F32, name=f"yt0{h}", tag=f"bank{h}") for h in range(2)]
-                yt = [halves[c // 2][:, c % 2, :] for c in range(4)]
-            else:
-                whole = ps.tile([P, 4, P], F32, name="yt1", tag="bank2")
-                yt = [whole[:, c, :] for c in range(4)]
-            for c in range(4):
-                cols = slice(c * P, (c + 1) * P)
-                nc.tensor.matmul_mx(out=yt[c], lhsT=xw[:, cols].bitcast(FP8X4), lhsT_scale=xs[:, cols],
-                                    rhs=wq[b][:].bitcast(FP8X4), rhs_scale=ws[b][:], start=True, stop=True)
-            back = [ps.tile([P, 2, P], F32, name=f"back{b}{h}", tag=f"bank{2 + 2 * b + h}") for h in range(2)]
-            for c in range(4):
-                z = sb.tile([P, P], F32, name=f"z{b}{c}")
-                nc.scalar.activation(z[:], yt[c], COPY, scale=new_col[:, c : c + 1])
-                nc.tensor.transpose(back[c // 2][:, c % 2, :], z[:], ident[:])
-            fresh = sb.tile([P, T], F32, name=f"fresh{b}")
-            for h in range(2):
-                nc.scalar.copy(fresh[:, h * 2 * P : (h + 1) * 2 * P], back[h][:].rearrange("p c n -> p (c n)"))
-            nc.vector.tensor_tensor(mems[b][:].indirect(offs[:]), kept[b][:], fresh[:], ADD)
             nc.sync.dma_start(out[b * P : (b + 1) * P, :], mems[b][:])

@@ -49,16 +49,16 @@ def tile_picked_wema_none_l_kernel(tc, x_words, x_scales, mem, w1, old, new, slo
             rows = slice(32 * q, 32 * q + 32)
             nc.vector.tensor_tensor(ident[rows, rows], ramp[rows, :], turned[rows, :], mybir.AluOpType.is_equal)
 
-        nc.sync.dma_start(old_col[:], old[0, :].rearrange("(p b) -> p b", b=4))
+        nc.scalar.dma_start(old_col[:], old[0, :].rearrange("(p b) -> p b", b=4))
         nc.sync.dma_start(offs[:], slot)
-        nc.sync.dma_start(new_rows[:], new[0:8, :].rearrange("u (c q i) -> q (u c) i", c=4, q=4))
+        nc.scalar.dma_start(new_rows[:], new[0:8, :].rearrange("u (c q i) -> q (u c) i", c=4, q=4))
         nc.sync.dma_start(w_raw[:], w1.rearrange("(p j) n -> p j n", j=PACK))
+        nc.sync.dma_start(mems[0][:], mem[0:P, :])
         nc.sync.dma_start(xs[0:4, :].bitcast(I32), x_scales[0, 0:4, :].bitcast(I32))
         nc.sync.dma_start(xs[32:36, :].bitcast(I32), x_scales[0, 4:8, :].bitcast(I32))
-        nc.sync.dma_start(xw[0][:].bitcast(I32), words[:, 0:FIRST])
-        nc.sync.dma_start(mems[0][:], mem[0:P, :])
         nc.sync.dma_start(xs[64:68, :].bitcast(I32), x_scales[0, 8:12, :].bitcast(I32))
         nc.sync.dma_start(xs[96:100, :].bitcast(I32), x_scales[0, 12:16, :].bitcast(I32))
+        nc.sync.dma_start(xw[0][:].bitcast(I32), words[:, 0:FIRST])
         nc.sync.dma_start(mems[1][:], mem[P : 2 * P, :])
         nc.sync.dma_start(xw[1][:].bitcast(I32), words[:, FIRST:T])
 

@@ -53,10 +53,10 @@ def tile_picked_wema_none_l_kernel(tc, x_words, x_scales, mem, w1, old, new, slo
         nc.sync.dma_start(offs[:], slot)
         nc.scalar.dma_start(new_rows[:], new[0:8, :].rearrange("u (c q i) -> q (u c) i", c=4, q=4))
         nc.sync.dma_start(w_raw[:], w1.rearrange("(p j) n -> p j n", j=PACK))
+        nc.scalar.dma_start(xs[0:4, :].bitcast(I32), x_scales[0, 0:4, :].bitcast(I32))
+        nc.scalar.dma_start(xs[32:36, :].bitcast(I32), x_scales[0, 4:8, :].bitcast(I32))
         nc.sync.dma_start(mems[0][:], mem[0:P, :])
-        nc.sync.dma_start(xs[0:4, :].bitcast(I32), x_scales[0, 0:4, :].bitcast(I32))
-        nc.sync.dma_start(xs[32:36, :].bitcast(I32), x_scales[0, 4:8, :].bitcast(I32))
-        nc.sync.dma_start(xs[64:68, :].bitcast(I32), x_scales[0, 8:12, :].bitcast(I32))
+        nc.scalar.dma_start(xs[64:68, :].bitcast(I32), x_scales[0, 8:12, :].bitcast(I32))
         nc.sync.dma_start(xs[96:100, :].bitcast(I32), x_scales[0, 12:16, :].bitcast(I32))
         nc.sync.dma_start(xw[0][:].bitcast(I32), words[:, 0:FIRST])
         nc.sync.dma_start(mems[1][:], mem[P : 2 * P, :])

@@ -37,17 +37,17 @@ def tile_picked_wema_none_l_kernel(tc, x_words, x_scales, mem, w1, old, new, slo
         ident = sb.tile([P, P], F32, name="ident")
         words = x_words[0].rearrange("p n t -> p (n t)").bitcast(I32)
 
-        nc.gpsimd.memset(xs[:].bitcast(I32), 0)
-        ones = sb.tile([P, 32], F32, name="ones")
-        ramp = sb.tile([P, 32], F32, name="ramp", align_bytes=64)
+        nc.vector.memset(xs[:].bitcast(I32), 0)
+        first = sb.tile([P, 1], F32, name="first")
+        for q in range(4):
+            nc.gpsimd.memset(first[32 * q : 32 * q + 32, :], 32.0 * q)
+        ones = sb.tile([P, P], F32, name="ones")
+        ramp = sb.tile([P, P], F32, name="ramp", align_bytes=64)
         turned = sb.tile([P, 32], F32, name="turned", align_bytes=64)
         nc.vector.memset(ones[:], 1.0)
-        nc.vector.memset(ident[:], 0.0)
         nc.vector.tensor_tensor_scan(ramp[:], ones[:], ones[:], 0.0, MULT, ADD)
-        nc.vector.transpose(turned[:], ramp[:])
-        for q in range(4):
-            rows = slice(32 * q, 32 * q + 32)
-            nc.vector.tensor_tensor(ident[rows, rows], ramp[rows, :], turned[rows, :], mybir.AluOpType.is_equal)
+        nc.vector.transpose(turned[:], ramp[:, 0:32])
+        nc.vector.tensor_scalar(ident[:], ramp[:], first[:], turned[:, 0:1], mybir.AluOpType.subtract, mybir.AluOpType.is_equal)
 
         nc.scalar.dma_start(old_col[:], old[0, :].rearrange("(p b) -> p b", b=4))
         nc.sync.dma_start(offs[:], slot)
@@ -66,7 +66,8 @@ def tile_picked_wema_none_l_kernel(tc, x_words, x_scales, mem, w1, old, new, slo
         for b in range(4):
             nc.tensor.transpose(old_ps[:, b, :], old_col[:, b : b + 1].to_broadcast([P, P]), ident[:])
         old_sb = sb.tile([P, T], F32, name="old_sb")
-        nc.scalar.copy(old_sb[:].rearrange("p (n b) -> p n b", b=4), old_ps[:].rearrange("p b n -> p n b"))
+        for h in range(2):
+            nc.scalar.copy(old_sb[:, h * N : (h + 1) * N].rearrange("p (n b) -> p n b", b=4), old_ps[:, :, h * 64 : (h + 1) * 64].rearrange("p b n -> p n b"))
         new_col = sb.tile([P, 32], F32, name="new_col", align_bytes=64)
         nc.vector.transpose(new_col[:], new_rows[:])
 
@@ -83,8 +84,8 @@ def tile_picked_wema_none_l_kernel(tc, x_words, x_scales, mem, w1, old, new, slo
             nc.vector.quantize_mx(out=wq[:, rows].bitcast(FP8X4), scales=ws[:, rows], in_=grouped[b][:].rearrange("p n t -> p (n t)"))
 
         kept = [sb.tile([P, T], F32, name=f"kept{b}") for b in range(2)]
-        for b in range(2):
-            nc.vector.tensor_tensor(kept[b][:], mems[b][:].indirect(offs[:]), old_sb[:], MULT)
+        for b, lo, hi in [(0, 0, N), (0, N, T), (1, 0, T)]:
+            nc.vector.tensor_tensor(kept[b][:, lo:hi], mems[b][:].indirect(offs[:, lo // 16 : hi // 16]), old_sb[:, lo:hi], MULT)
 
         for lo, hi in [(0, P), (P, 2 * P), (2 * P, T)]:
             chunks = (hi - lo) // P

@@ -49,20 +49,20 @@ def tile_picked_wema_none_l_kernel(tc, x_words, x_scales, mem, w1, old, new, slo
         nc.vector.transpose(turned[:], ramp[:, 0:32])
         nc.vector.tensor_scalar(ident[:], ramp[:], first[:], turned[:, 0:1], mybir.AluOpType.subtract, mybir.AluOpType.is_equal)
 
-        nc.scalar.dma_start(old_col[:], old[0, :].rearrange("(p b) -> p b", b=4))
-        nc.sync.dma_start(offs[:], slot)
+        nc.sync.dma_start(old_col[:], old[0, :].rearrange("(p b) -> p b", b=4))
         nc.scalar.dma_start(new_rows[:], new[0:8, :].rearrange("u (c q i) -> q (u c) i", c=4, q=4))
+        nc.gpsimd.dma_start(xs[96:100, :].bitcast(I32), x_scales[0, 12:16, :].bitcast(I32))
         nc.sync.dma_start(w_raw[:], w1.rearrange("(p j) n -> p j n", j=PACK))
         nc.scalar.dma_start(xs[0:4, :].bitcast(I32), x_scales[0, 0:4, :].bitcast(I32))
         nc.scalar.dma_start(xs[32:36, :].bitcast(I32), x_scales[0, 4:8, :].bitcast(I32))
-        nc.sync.dma_start(mems[0][:], mem[0:P, :])
         nc.scalar.dma_start(xs[64:68, :].bitcast(I32), x_scales[0, 8:12, :].bitcast(I32))
-        nc.sync.dma_start(xs[96:100, :].bitcast(I32), x_scales[0, 12:16, :].bitcast(I32))
+        nc.sync.dma_start(offs[:], slot)
+        nc.sync.dma_start(mems[0][:], mem[0:P, :])
         nc.sync.dma_start(xw[0][:].bitcast(I32), words[:, 0:FIRST])
         nc.sync.dma_start(mems[1][:], mem[P : 2 * P, :])
         nc.sync.dma_start(xw[1][:].bitcast(I32), words[:, FIRST:T])
 
-        old_ps = ps.tile([P, 4, P], F32, name="old_ps", tag="product0")
+        old_ps = ps.tile([P, 4, P], F32, name="old_ps", tag="bank0")
         for b in range(4):
             nc.tensor.transpose(old_ps[:, b, :], old_col[:, b : b + 1].to_broadcast([P, P]), ident[:])
         old_sb = sb.tile([P, T], F32, name="old_sb")
@@ -87,22 +87,30 @@ def tile_picked_wema_none_l_kernel(tc, x_words, x_scales, mem, w1, old, new, slo
         for b, lo, hi in [(0, 0, N), (0, N, T), (1, 0, T)]:
             nc.vector.tensor_tensor(kept[b][:, lo:hi], mems[b][:].indirect(offs[:, lo // 16 : hi // 16]), old_sb[:, lo:hi], MULT)
 
-        for lo, hi in [(0, P), (P, 2 * P), (2 * P, T)]:
-            chunks = (hi - lo) // P
-            backs = [ps.tile([P, chunks, P], F32, name=f"back{b}{lo}", tag=f"back{b}{lo // P % 2}") for b in range(2)]
-            for i in range(chunks):
-                c = lo // P + i
-                yt = ps.tile([P, N], F32, name=f"yt{c}", tag=f"product{c}")
-                nc.tensor.matmul_mx(out=yt[:], lhsT=(xw[0][:] if c == 0 else xw[1][:, (c - 1) * P : c * P]).bitcast(FP8X4), lhsT_scale=xs[:, c * P : (c + 1) * P],
-                                    rhs=wq[:].bitcast(FP8X4), rhs_scale=ws[:], start=True, stop=True)
-                z = sb.tile([P, N], F32, name=f"z{c}")
-                for cols in ([slice(0, P), slice(P, N)] if c == 0 else [slice(0, N)]):
-                    nc.scalar.activation(z[:, cols], yt[:, cols], COPY, scale=new_col[:, c : c + 1])
-                for b in range(2):
-                    nc.tensor.transpose(backs[b][:, i, :], z[:, b * P : (b + 1) * P], ident[:])
+        def product(c, cols, bank):
+            yt = ps.tile([P, cols.stop - cols.start], F32, name=f"yt{c}_{cols.start}", tag=f"bank{bank}")
+            nc.tensor.matmul_mx(out=yt[:], lhsT=(xw[0][:] if c == 0 else xw[1][:, (c - 1) * P : c * P]).bitcast(FP8X4), lhsT_scale=xs[:, c * P : (c + 1) * P],
+                                rhs=wq[:, cols].bitcast(FP8X4), rhs_scale=ws[:, cols], start=True, stop=True)
+            z = sb.tile([P, cols.stop - cols.start], F32, name=f"z{c}_{cols.start}")
+            nc.scalar.activation(z[:], yt[:], COPY, scale=new_col[:, c : c + 1])
+            return z
+
+        def put(b, lo, scaled, bank):
+            hi = lo + P * len(scaled)
+            back = ps.tile([P, len(scaled), P], F32, name=f"back{b}_{lo}", tag=f"bank{bank}")
+            for i, z in enumerate(scaled):
+                nc.tensor.transpose(back[:, i, :], z, ident[:])
+            fresh = sb.tile([P, hi - lo], F32, name=f"fresh{b}_{lo}")
+            nc.scalar.copy(fresh[:], back[:].rearrange("p c n -> p (c n)"))
+            nc.vector.tensor_tensor(mems[b][:].indirect(offs[:, lo // 16 : hi // 16]), kept[b][:, lo:hi], fresh[:], ADD)
+            return fresh
+
+        for c in range(2):
+            scaled = [product(c, slice(b * P, (b + 1) * P), 4 * c + b) for b in range(2)]
             for b in range(2):
-                fresh = sb.tile([P, hi - lo], F32, name=f"fresh{b}{lo}")
-                nc.scalar.copy(fresh[:], backs[b][:].rearrange("p c n -> p (c n)"))
-                nc.vector.tensor_tensor(mems[b][:].indirect(offs[:, lo // 16 : hi // 16]), kept[b][:, lo:hi], fresh[:], ADD)
+                put(b, c * P, [scaled[b][:]], 4 * c + 2 + b)
+        scaled = [product(c, slice(0, N), c - 2) for c in (2, 3)]
+        for b in range(2):
+            put(b, 2 * P, [z[:, b * P : (b + 1) * P] for z in scaled], 2 + b)
         for b in range(2):
             nc.sync.dma_start(out[b * P : (b + 1) * P, :], mems[b][:])

@@ -37,6 +37,7 @@ def tile_picked_wema_none_l_kernel(tc, x_words, x_scales, mem, w1, old, new, slo
         ident = sb.tile([P, P], F32, name="ident")
         words = x_words[0].rearrange("p n t -> p (n t)").bitcast(I32)
 
+        nc.gpsimd.dma_start(xw[0][:].bitcast(I32), words[:, 0:FIRST])
         nc.vector.memset(xs[:].bitcast(I32), 0)
         first = sb.tile([P, 1], F32, name="first")
         for q in range(4):
@@ -51,14 +52,13 @@ def tile_picked_wema_none_l_kernel(tc, x_words, x_scales, mem, w1, old, new, slo
 
         nc.sync.dma_start(old_col[:], old[0, :].rearrange("(p b) -> p b", b=4))
         nc.scalar.dma_start(new_rows[:], new[0:8, :].rearrange("u (c q i) -> q (u c) i", c=4, q=4))
-        nc.gpsimd.dma_start(xs[96:100, :].bitcast(I32), x_scales[0, 12:16, :].bitcast(I32))
         nc.sync.dma_start(w_raw[:], w1.rearrange("(p j) n -> p j n", j=PACK))
         nc.scalar.dma_start(xs[0:4, :].bitcast(I32), x_scales[0, 0:4, :].bitcast(I32))
         nc.scalar.dma_start(xs[32:36, :].bitcast(I32), x_scales[0, 4:8, :].bitcast(I32))
         nc.scalar.dma_start(xs[64:68, :].bitcast(I32), x_scales[0, 8:12, :].bitcast(I32))
         nc.sync.dma_start(offs[:], slot)
         nc.sync.dma_start(mems[0][:], mem[0:P, :])
-        nc.sync.dma_start(xw[0][:].bitcast(I32), words[:, 0:FIRST])
+        nc.sync.dma_start(xs[96:100, :].bitcast(I32), x_scales[0, 12:16, :].bitcast(I32))
         nc.sync.dma_start(mems[1][:], mem[P : 2 * P, :])
         nc.sync.dma_start(xw[1][:].bitcast(I32), words[:, FIRST:T])
 

@@ -6,7 +6,6 @@ K, T, N, U = 512, 512, 256, 1024
 FLOPS = 2 * K * T * N
 P = 128
 PACK = 4
-FIRST = 128
 
 F32 = mybir.dt.float32
 BF16 = mybir.dt.bfloat16
@@ -26,91 +25,93 @@ def tile_picked_wema_none_l_kernel(tc, x_words, x_scales, mem, w1, old, new, slo
         sb = ctx.enter_context(tc.tile_pool(name="sb", bufs=1))
         ps = ctx.enter_context(tc.psum_pool(name="ps", bufs=1))
 
-        pieces = [(0, FIRST), (FIRST, T)]
         offs = sb.tile([P, T // 16], U16, name="offs")
-        mems = [sb.tile([P, U], F32, name=f"mem{b}") for b in range(2)]
-        w_raw = sb.tile([P, PACK, N], F32, name="w_raw")
-        xw = [sb.tile([P, hi - lo], U32, name=f"xw{lo}", align_bytes=64) for lo, hi in pieces]
+        w_raw = sb.tile([P, PACK, N], F32, name="w_raw", tag="w_raw", align_bytes=64)
+        xw = sb.tile([P, T], U32, name="xw", align_bytes=64)
         xs = sb.tile([P, T], U8, name="xs", align_bytes=64)
         old_col = sb.tile([P, 4], F32, name="old_col")
         new_rows = sb.tile([P, 32], F32, name="new_rows", align_bytes=64)
         ident = sb.tile([P, P], F32, name="ident")
-        words = x_words[0].rearrange("p n t -> p (n t)").bitcast(I32)
 
-        nc.gpsimd.dma_start(xw[0][:].bitcast(I32), words[:, 0:FIRST])
-        nc.vector.memset(xs[:].bitcast(I32), 0)
+        nc.gpsimd.dma_start(new_rows[:], new[0:8, :].rearrange("u (c q i) -> q (u c) i", c=4, q=4))
         first = sb.tile([P, 1], F32, name="first")
         for q in range(4):
-            nc.gpsimd.memset(first[32 * q : 32 * q + 32, :], 32.0 * q)
+            engine = nc.gpsimd if q == 0 else nc.vector
+            engine.memset(first[32 * q : 32 * q + 32, :], 32.0 * q)
         ones = sb.tile([P, P], F32, name="ones")
-        ramp = sb.tile([P, P], F32, name="ramp", align_bytes=64)
+        ramp = sb.tile([P, P], F32, name="ramp", tag="mem0", align_bytes=64)
         turned = sb.tile([P, 32], F32, name="turned", align_bytes=64)
         nc.vector.memset(ones[:], 1.0)
         nc.vector.tensor_tensor_scan(ramp[:], ones[:], ones[:], 0.0, MULT, ADD)
         nc.vector.transpose(turned[:], ramp[:, 0:32])
         nc.vector.tensor_scalar(ident[:], ramp[:], first[:], turned[:, 0:1], mybir.AluOpType.subtract, mybir.AluOpType.is_equal)
 
+        mems = [sb.tile([P, U], F32, name=f"mem{b}", tag=f"mem{b}", align_bytes=64) for b in range(2)]
+        new_sb = sb.tile([P, T], F32, name="new_sb")
         nc.sync.dma_start(old_col[:], old[0, :].rearrange("(p b) -> p b", b=4))
-        nc.scalar.dma_start(new_rows[:], new[0:8, :].rearrange("u (c q i) -> q (u c) i", c=4, q=4))
+        for q in range(4):
+            rows = x_scales[0, 4 * q : 4 * q + 4, :].bitcast(I32)
+            nc.scalar.dma_start(xs[32 * q : 32 * q + 32, :].bitcast(I32), rows.unsqueeze(0).to_broadcast([8, 4, T // 4]))
         nc.sync.dma_start(w_raw[:], w1.rearrange("(p j) n -> p j n", j=PACK))
-        nc.scalar.dma_start(xs[0:4, :].bitcast(I32), x_scales[0, 0:4, :].bitcast(I32))
-        nc.scalar.dma_start(xs[32:36, :].bitcast(I32), x_scales[0, 4:8, :].bitcast(I32))
-        nc.scalar.dma_start(xs[64:68, :].bitcast(I32), x_scales[0, 8:12, :].bitcast(I32))
-        nc.sync.dma_start(offs[:], slot)
+        nc.sync.dma_start(xw[:].bitcast(I32), x_words[0].rearrange("p n t -> p (n t)").bitcast(I32))
         nc.sync.dma_start(mems[0][:], mem[0:P, :])
-        nc.sync.dma_start(xs[96:100, :].bitcast(I32), x_scales[0, 12:16, :].bitcast(I32))
+        nc.sync.dma_start(offs[:], slot)
+        nc.sync.dma_start(new_sb[:], new)
         nc.sync.dma_start(mems[1][:], mem[P : 2 * P, :])
-        nc.sync.dma_start(xw[1][:].bitcast(I32), words[:, FIRST:T])
 
         old_ps = ps.tile([P, 4, P], F32, name="old_ps", tag="bank0")
         for b in range(4):
             nc.tensor.transpose(old_ps[:, b, :], old_col[:, b : b + 1].to_broadcast([P, P]), ident[:])
         old_sb = sb.tile([P, T], F32, name="old_sb")
-        for h in range(2):
-            nc.scalar.copy(old_sb[:, h * N : (h + 1) * N].rearrange("p (n b) -> p n b", b=4), old_ps[:, :, h * 64 : (h + 1) * 64].rearrange("p b n -> p n b"))
-        new_col = sb.tile([P, 32], F32, name="new_col", align_bytes=64)
-        nc.vector.transpose(new_col[:], new_rows[:])
+        nc.scalar.copy(old_sb[:].rearrange("p (n b) -> p n b", b=4), old_ps[:].rearrange("p b n -> p n b"))
 
         grouped = [sb.tile([P, P, PACK], BF16, name=f"grouped{b}", align_bytes=64) for b in range(2)]
-        wq = sb.tile([P, N], U32, name="wq", align_bytes=64)
-        ws = sb.tile([P, N], U8, name="ws", align_bytes=64)
+        wq = [sb.tile([P, P], U32, name=f"wq{b}", align_bytes=64) for b in range(2)]
+        ws = [sb.tile([P, P], U8, name=f"ws{b}", align_bytes=64) for b in range(2)]
         for b in range(2):
             nc.vector.tensor_copy(
                 grouped[b][:].rearrange("p (c i) t -> p c t i", i=4),
                 w_raw[:, :, b * P : (b + 1) * P].rearrange("p t (c i) -> p c t i", i=4),
             )
+        new_col = sb.tile([P, 32], F32, name="new_col", tag="w_raw", align_bytes=64)
+        nc.vector.transpose(new_col[:], new_rows[:])
         for b in range(2):
-            rows = slice(b * P, (b + 1) * P)
-            nc.vector.quantize_mx(out=wq[:, rows].bitcast(FP8X4), scales=ws[:, rows], in_=grouped[b][:].rearrange("p n t -> p (n t)"))
+            nc.vector.quantize_mx(out=wq[b][:].bitcast(FP8X4), scales=ws[b][:], in_=grouped[b][:].rearrange("p n t -> p (n t)"))
 
         kept = [sb.tile([P, T], F32, name=f"kept{b}") for b in range(2)]
-        for b, lo, hi in [(0, 0, N), (0, N, T), (1, 0, T)]:
+
+        def fetch(b, lo, hi):
             nc.vector.tensor_tensor(kept[b][:, lo:hi], mems[b][:].indirect(offs[:, lo // 16 : hi // 16]), old_sb[:, lo:hi], MULT)
 
-        def product(c, cols, bank):
-            yt = ps.tile([P, cols.stop - cols.start], F32, name=f"yt{c}_{cols.start}", tag=f"bank{bank}")
-            nc.tensor.matmul_mx(out=yt[:], lhsT=(xw[0][:] if c == 0 else xw[1][:, (c - 1) * P : c * P]).bitcast(FP8X4), lhsT_scale=xs[:, c * P : (c + 1) * P],
-                                rhs=wq[:, cols].bitcast(FP8X4), rhs_scale=ws[:, cols], start=True, stop=True)
-            z = sb.tile([P, cols.stop - cols.start], F32, name=f"z{c}_{cols.start}")
+        fetch(0, 0, N)
+        fetch(0, N, T)
+
+        scaled = []
+        for c in range(4):
+            yt = ps.tile([P, P], F32, name=f"yt{c}", tag=f"bank{2 + c}")
+            nc.tensor.matmul_mx(out=yt[:], lhsT=xw[:, c * P : (c + 1) * P].bitcast(FP8X4), lhsT_scale=xs[:, c * P : (c + 1) * P],
+                                rhs=wq[0][:].bitcast(FP8X4), rhs_scale=ws[0][:], start=True, stop=True)
+            z = sb.tile([P, P], F32, name=f"z{c}")
             nc.scalar.activation(z[:], yt[:], COPY, scale=new_col[:, c : c + 1])
-            return z
+            scaled.append(z)
+        y1 = ps.tile([P, T], F32, name="y1", tag="bank1")
+        nc.tensor.matmul_mx(out=y1[:], lhsT=wq[1][:].bitcast(FP8X4), lhsT_scale=ws[1][:], rhs=xw[:].bitcast(FP8X4), rhs_scale=xs[:], start=True, stop=True)
 
-        def put(b, lo, scaled, bank):
-            hi = lo + P * len(scaled)
-            back = ps.tile([P, len(scaled), P], F32, name=f"back{b}_{lo}", tag=f"bank{bank}")
-            for i, z in enumerate(scaled):
-                nc.tensor.transpose(back[:, i, :], z, ident[:])
-            fresh = sb.tile([P, hi - lo], F32, name=f"fresh{b}_{lo}")
-            nc.scalar.copy(fresh[:], back[:].rearrange("p c n -> p (c n)"))
-            nc.vector.tensor_tensor(mems[b][:].indirect(offs[:, lo // 16 : hi // 16]), kept[b][:, lo:hi], fresh[:], ADD)
-            return fresh
+        def put(lo, hi, bank, total):
+            back = ps.tile([P, hi - lo, P], F32, name=f"back{lo}", tag=f"bank{bank}")
+            for c in range(lo, hi):
+                nc.tensor.transpose(back[:, c - lo, :], scaled[c][:], ident[:])
+            nc.vector.tensor_tensor(total, back[:].rearrange("p c n -> p (c n)"), kept[0][:, lo * P : hi * P], ADD)
+            nc.scalar.activation(mems[0][:].indirect(offs[:, lo * 8 : hi * 8]), total, COPY)
 
-        for c in range(2):
-            scaled = [product(c, slice(b * P, (b + 1) * P), 4 * c + b) for b in range(2)]
-            for b in range(2):
-                put(b, c * P, [scaled[b][:]], 4 * c + 2 + b)
-        scaled = [product(c, slice(0, N), c - 2) for c in (2, 3)]
-        for b in range(2):
-            put(b, 2 * P, [z[:, b * P : (b + 1) * P] for z in scaled], 2 + b)
+        sums = sb.tile([P, 3 * P], F32, name="sums")
+        put(0, 1, 7, sums[:, 0:P])
+        put(1, 3, 0, sums[:, P : 3 * P])
+        fresh = sb.tile([P, T], F32, name="fresh")
+        nc.vector.tensor_tensor(fresh[:], y1[:], new_sb[:], MULT)
+        fetch(1, 0, N)
+        fetch(1, N, T)
+        put(3, 4, 6, old_sb[:, 0:P])
+        nc.vector.tensor_tensor(mems[1][:].indirect(offs[:]), kept[1][:], fresh[:], ADD)
         for b in range(2):
             nc.sync.dma_start(out[b * P : (b + 1) * P, :], mems[b][:])

@@ -26,33 +26,32 @@ def tile_picked_wema_none_l_kernel(tc, x_words, x_scales, mem, w1, old, new, slo
         ps = ctx.enter_context(tc.psum_pool(name="ps", bufs=1))
 
         offs = sb.tile([P, T // 16], U16, name="offs")
-        w_raw = sb.tile([P, PACK, N], F32, name="w_raw", tag="w_raw", align_bytes=64)
+        w_raw = sb.tile([P, PACK, N], F32, name="w_raw")
         xw = sb.tile([P, T], U32, name="xw", align_bytes=64)
         xs = sb.tile([P, T], U8, name="xs", align_bytes=64)
         old_col = sb.tile([P, 4], F32, name="old_col")
         new_rows = sb.tile([P, 32], F32, name="new_rows", align_bytes=64)
         ident = sb.tile([P, P], F32, name="ident")
 
-        nc.gpsimd.dma_start(new_rows[:], new[0:8, :].rearrange("u (c q i) -> q (u c) i", c=4, q=4))
+        nc.vector.memset(xs[:].bitcast(I32), 0)
         first = sb.tile([P, 1], F32, name="first")
         for q in range(4):
-            engine = nc.gpsimd if q == 0 else nc.vector
-            engine.memset(first[32 * q : 32 * q + 32, :], 32.0 * q)
+            nc.gpsimd.memset(first[32 * q : 32 * q + 32, :], 32.0 * q)
         ones = sb.tile([P, P], F32, name="ones")
-        ramp = sb.tile([P, P], F32, name="ramp", tag="mem0", align_bytes=64)
+        ramp = sb.tile([P, P], F32, name="ramp", align_bytes=64)
         turned = sb.tile([P, 32], F32, name="turned", align_bytes=64)
         nc.vector.memset(ones[:], 1.0)
         nc.vector.tensor_tensor_scan(ramp[:], ones[:], ones[:], 0.0, MULT, ADD)
         nc.vector.transpose(turned[:], ramp[:, 0:32])
         nc.vector.tensor_scalar(ident[:], ramp[:], first[:], turned[:, 0:1], mybir.AluOpType.subtract, mybir.AluOpType.is_equal)
 
-        mems = [sb.tile([P, U], F32, name=f"mem{b}", tag=f"mem{b}", align_bytes=64) for b in range(2)]
+        mems = [sb.tile([P, U], F32, name=f"mem{b}") for b in range(2)]
         new_sb = sb.tile([P, T], F32, name="new_sb")
         nc.sync.dma_start(old_col[:], old[0, :].rearrange("(p b) -> p b", b=4))
-        for q in range(4):
-            rows = x_scales[0, 4 * q : 4 * q + 4, :].bitcast(I32)
-            nc.scalar.dma_start(xs[32 * q : 32 * q + 32, :].bitcast(I32), rows.unsqueeze(0).to_broadcast([8, 4, T // 4]))
+        nc.scalar.dma_start(new_rows[:], new[0:8, :].rearrange("u (c q i) -> q (u c) i", c=4, q=4))
         nc.sync.dma_start(w_raw[:], w1.rearrange("(p j) n -> p j n", j=PACK))
+        for q in range(4):
+            nc.scalar.dma_start(xs[32 * q : 32 * q + 4, :].bitcast(I32), x_scales[0, 4 * q : 4 * q + 4, :].bitcast(I32))
         nc.sync.dma_start(xw[:].bitcast(I32), x_words[0].rearrange("p n t -> p (n t)").bitcast(I32))
         nc.sync.dma_start(mems[0][:], mem[0:P, :])
         nc.sync.dma_start(offs[:], slot)
@@ -73,7 +72,7 @@ def tile_picked_wema_none_l_kernel(tc, x_words, x_scales, mem, w1, old, new, slo
                 grouped[b][:].rearrange("p (c i) t -> p c t i", i=4),
                 w_raw[:, :, b * P : (b + 1) * P].rearrange("p t (c i) -> p c t i", i=4),
             )
-        new_col = sb.tile([P, 32], F32, name="new_col", tag="w_raw", align_bytes=64)
+        new_col = sb.tile([P, 32], F32, name="new_col", align_bytes=64)
         nc.vector.transpose(new_col[:], new_rows[:])
         for b in range(2):
             nc.vector.quantize_mx(out=wq[b][:].bitcast(FP8X4), scales=ws[b][:], in_=grouped[b][:].rearrange("p n t -> p (n t)"))

@@ -46,7 +46,7 @@ def tile_picked_wema_none_l_kernel(tc, x_words, x_scales, mem, w1, old, new, slo
         nc.vector.tensor_scalar(ident[:], ramp[:], first[:], turned[:, 0:1], mybir.AluOpType.subtract, mybir.AluOpType.is_equal)
 
         mems = [sb.tile([P, U], F32, name=f"mem{b}") for b in range(2)]
-        new_sb = sb.tile([P, T], F32, name="new_sb")
+        new_sb = sb.tile([P, N], F32, name="new_sb")
         nc.sync.dma_start(old_col[:], old[0, :].rearrange("(p b) -> p b", b=4))
         nc.scalar.dma_start(new_rows[:], new[0:8, :].rearrange("u (c q i) -> q (u c) i", c=4, q=4))
         nc.sync.dma_start(w_raw[:], w1.rearrange("(p j) n -> p j n", j=PACK))
@@ -55,7 +55,7 @@ def tile_picked_wema_none_l_kernel(tc, x_words, x_scales, mem, w1, old, new, slo
         nc.sync.dma_start(xw[:].bitcast(I32), x_words[0].rearrange("p n t -> p (n t)").bitcast(I32))
         nc.sync.dma_start(mems[0][:], mem[0:P, :])
         nc.sync.dma_start(offs[:], slot)
-        nc.sync.dma_start(new_sb[:], new)
+        nc.sync.dma_start(new_sb[:], new[:, 0:N])
         nc.sync.dma_start(mems[1][:], mem[P : 2 * P, :])
 
         old_ps = ps.tile([P, 4, P], F32, name="old_ps", tag="bank0")
@@ -65,8 +65,8 @@ def tile_picked_wema_none_l_kernel(tc, x_words, x_scales, mem, w1, old, new, slo
         nc.scalar.copy(old_sb[:].rearrange("p (n b) -> p n b", b=4), old_ps[:].rearrange("p b n -> p n b"))
 
         grouped = [sb.tile([P, P, PACK], BF16, name=f"grouped{b}", align_bytes=64) for b in range(2)]
-        wq = [sb.tile([P, P], U32, name=f"wq{b}", align_bytes=64) for b in range(2)]
-        ws = [sb.tile([P, P], U8, name=f"ws{b}", align_bytes=64) for b in range(2)]
+        wq = sb.tile([P, N], U32, name="wq", align_bytes=64)
+        ws = sb.tile([P, N], U8, name="ws", align_bytes=64)
         for b in range(2):
             nc.vector.tensor_copy(
                 grouped[b][:].rearrange("p (c i) t -> p c t i", i=4),
@@ -75,7 +75,8 @@ def tile_picked_wema_none_l_kernel(tc, x_words, x_scales, mem, w1, old, new, slo
         new_col = sb.tile([P, 32], F32, name="new_col", align_bytes=64)
         nc.vector.transpose(new_col[:], new_rows[:])
         for b in range(2):
-            nc.vector.quantize_mx(out=wq[b][:].bitcast(FP8X4), scales=ws[b][:], in_=grouped[b][:].rearrange("p n t -> p (n t)"))
+            rows = slice(b * P, (b + 1) * P)
+            nc.vector.quantize_mx(out=wq[:, rows].bitcast(FP8X4), scales=ws[:, rows], in_=grouped[b][:].rearrange("p n t -> p (n t)"))
 
         kept = [sb.tile([P, T], F32, name=f"kept{b}") for b in range(2)]
 
@@ -83,34 +84,41 @@ def tile_picked_wema_none_l_kernel(tc, x_words, x_scales, mem, w1, old, new, slo
             nc.vector.tensor_tensor(kept[b][:, lo:hi], mems[b][:].indirect(offs[:, lo // 16 : hi // 16]), old_sb[:, lo:hi], MULT)
 
         fetch(0, 0, N)
-        fetch(0, N, T)
+        fetch(0, N, 3 * P)
 
         scaled = []
         for c in range(4):
-            yt = ps.tile([P, P], F32, name=f"yt{c}", tag=f"bank{2 + c}")
+            width = P if c < 2 else N
+            yt = ps.tile([P, width], F32, name=f"yt{c}", tag=f"bank{2 + c}")
             nc.tensor.matmul_mx(out=yt[:], lhsT=xw[:, c * P : (c + 1) * P].bitcast(FP8X4), lhsT_scale=xs[:, c * P : (c + 1) * P],
-                                rhs=wq[0][:].bitcast(FP8X4), rhs_scale=ws[0][:], start=True, stop=True)
-            z = sb.tile([P, P], F32, name=f"z{c}")
+                                rhs=wq[:, 0:width].bitcast(FP8X4), rhs_scale=ws[:, 0:width], start=True, stop=True)
+            z = sb.tile([P, width], F32, name=f"z{c}")
             nc.scalar.activation(z[:], yt[:], COPY, scale=new_col[:, c : c + 1])
             scaled.append(z)
-        y1 = ps.tile([P, T], F32, name="y1", tag="bank1")
-        nc.tensor.matmul_mx(out=y1[:], lhsT=wq[1][:].bitcast(FP8X4), lhsT_scale=ws[1][:], rhs=xw[:].bitcast(FP8X4), rhs_scale=xs[:], start=True, stop=True)
+        plain = sb.tile([P, P], F32, name="plain")
+        nc.scalar.activation(plain[:], mems[0][:].indirect(offs[:, 24:32]), COPY)
 
         def put(lo, hi, bank, total):
             back = ps.tile([P, hi - lo, P], F32, name=f"back{lo}", tag=f"bank{bank}")
             for c in range(lo, hi):
-                nc.tensor.transpose(back[:, c - lo, :], scaled[c][:], ident[:])
+                nc.tensor.transpose(back[:, c - lo, :], scaled[c][:, 0:P], ident[:])
             nc.vector.tensor_tensor(total, back[:].rearrange("p c n -> p (c n)"), kept[0][:, lo * P : hi * P], ADD)
             nc.scalar.activation(mems[0][:].indirect(offs[:, lo * 8 : hi * 8]), total, COPY)
 
-        sums = sb.tile([P, 3 * P], F32, name="sums")
-        put(0, 1, 7, sums[:, 0:P])
-        put(1, 3, 0, sums[:, P : 3 * P])
+        sums = sb.tile([P, N], F32, name="sums")
+        put(0, 2, 7, sums[:])
+        y1 = ps.tile([P, N], F32, name="y1", tag="bank1")
+        nc.tensor.matmul_mx(out=y1[:], lhsT=wq[:, P:N].bitcast(FP8X4), lhsT_scale=ws[:, P:N], rhs=xw[:, 0:N].bitcast(FP8X4), rhs_scale=xs[:, 0:N], start=True, stop=True)
+        nc.vector.tensor_tensor(kept[0][:, 3 * P : T], plain[:], old_sb[:, 3 * P : T], MULT)
         fresh = sb.tile([P, T], F32, name="fresh")
-        nc.vector.tensor_tensor(fresh[:], y1[:], new_sb[:], MULT)
+        nc.vector.tensor_tensor(fresh[:, 0:N], y1[:], new_sb[:], MULT)
+        turned_back = ps.tile([P, 2, P], F32, name="turned_back", tag="bank2")
+        for c in (2, 3):
+            nc.tensor.transpose(turned_back[:, c - 2, :], scaled[c][:, P:N], ident[:])
+        nc.scalar.copy(fresh[:, N:T], turned_back[:].rearrange("p c n -> p (c n)"))
         fetch(1, 0, N)
         fetch(1, N, T)
-        put(3, 4, 6, old_sb[:, 0:P])
+        put(2, 4, 6, old_sb[:, 0:N])
         nc.vector.tensor_tensor(mems[1][:].indirect(offs[:]), kept[1][:], fresh[:], ADD)
         for b in range(2):
             nc.sync.dma_start(out[b * P : (b + 1) * P, :], mems[b][:])

@@ -50,9 +50,15 @@ def tile_picked_wema_none_l_kernel(tc, x_words, x_scales, mem, w1, old, new, slo
         nc.sync.dma_start(old_col[:], old[0, :].rearrange("(p b) -> p b", b=4))
         nc.scalar.dma_start(new_rows[:], new[0:8, :].rearrange("u (c q i) -> q (u c) i", c=4, q=4))
         nc.sync.dma_start(w_raw[:], w1.rearrange("(p j) n -> p j n", j=PACK))
-        for q in range(4):
-            nc.scalar.dma_start(xs[32 * q : 32 * q + 4, :].bitcast(I32), x_scales[0, 4 * q : 4 * q + 4, :].bitcast(I32))
-        nc.sync.dma_start(xw[:].bitcast(I32), x_words[0].rearrange("p n t -> p (n t)").bitcast(I32))
+
+        def load_scales(queue, q):
+            queue.dma_start(xs[32 * q : 32 * q + 4, :].bitcast(I32), x_scales[0, 4 * q : 4 * q + 4, :].bitcast(I32))
+
+        load_scales(nc.scalar, 0)
+        nc.scalar.dma_start(xw[:].bitcast(I32), x_words[0].rearrange("p n t -> p (n t)").bitcast(I32))
+        load_scales(nc.scalar, 1)
+        load_scales(nc.sync, 3)
+        load_scales(nc.scalar, 2)
         nc.sync.dma_start(mems[0][:], mem[0:P, :])
         nc.sync.dma_start(offs[:], slot)
         nc.sync.dma_start(new_sb[:], new[:, 0:N])

@@ -30,13 +30,15 @@ def tile_picked_wema_none_l_kernel(tc, x_words, x_scales, mem, w1, old, new, slo
         xw = sb.tile([P, T], U32, name="xw", align_bytes=64)
         xs = sb.tile([P, T], U8, name="xs", align_bytes=64)
         old_col = sb.tile([P, 4], F32, name="old_col")
-        new_rows = sb.tile([P, 32], F32, name="new_rows", align_bytes=64)
+        new_rows = sb.tile([P, P], F32, name="new_rows")
         ident = sb.tile([P, P], F32, name="ident")
 
         nc.vector.memset(xs[:].bitcast(I32), 0)
         first = sb.tile([P, 1], F32, name="first")
         for q in range(4):
             nc.gpsimd.memset(first[32 * q : 32 * q + 32, :], 32.0 * q)
+        nc.gpsimd.memset(new_rows[0:96, :], 0.0)
+        nc.gpsimd.memset(new_rows[96 : P - 4, :], 0.0)
         ones = sb.tile([P, P], F32, name="ones")
         ramp = sb.tile([P, P], F32, name="ramp", align_bytes=64)
         turned = sb.tile([P, 32], F32, name="turned", align_bytes=64)
@@ -48,7 +50,7 @@ def tile_picked_wema_none_l_kernel(tc, x_words, x_scales, mem, w1, old, new, slo
         mems = [sb.tile([P, U], F32, name=f"mem{b}") for b in range(2)]
         new_sb = sb.tile([P, N], F32, name="new_sb")
         nc.sync.dma_start(old_col[:], old[0, :].rearrange("(p b) -> p b", b=4))
-        nc.scalar.dma_start(new_rows[:], new[0:8, :].rearrange("u (c q i) -> q (u c) i", c=4, q=4))
+        nc.scalar.dma_start(new_rows[P - 4 : P, :], new[0, :].rearrange("(c n) -> c n", n=P))
         nc.sync.dma_start(w_raw[:], w1.rearrange("(p j) n -> p j n", j=PACK))
 
         def load_scales(queue, q):
@@ -64,6 +66,10 @@ def tile_picked_wema_none_l_kernel(tc, x_words, x_scales, mem, w1, old, new, slo
         nc.sync.dma_start(new_sb[:], new[:, 0:N])
         nc.sync.dma_start(mems[1][:], mem[P : 2 * P, :])
 
+        new_ps = ps.tile([P, P], F32, name="new_ps", tag="bank7")
+        nc.tensor.transpose(new_ps[:], new_rows[:], ident[:])
+        new_col = sb.tile([P, 4], F32, name="new_col")
+        nc.vector.tensor_copy(new_col[:], new_ps[:, P - 4 : P])
         old_ps = ps.tile([P, 4, P], F32, name="old_ps", tag="bank0")
         for b in range(4):
             nc.tensor.transpose(old_ps[:, b, :], old_col[:, b : b + 1].to_broadcast([P, P]), ident[:])
@@ -78,8 +84,6 @@ def tile_picked_wema_none_l_kernel(tc, x_words, x_scales, mem, w1, old, new, slo
                 grouped[b][:].rearrange("p (c i) t -> p c t i", i=4),
                 w_raw[:, :, b * P : (b + 1) * P].rearrange("p t (c i) -> p c t i", i=4),
             )
-        new_col = sb.tile([P, 32], F32, name="new_col", align_bytes=64)
-        nc.vector.transpose(new_col[:], new_rows[:])
         for b in range(2):
             rows = slice(b * P, (b + 1) * P)
             nc.vector.quantize_mx(out=wq[:, rows].bitcast(FP8X4), scales=ws[:, rows], in_=grouped[b][:].rearrange("p n t -> p (n t)"))

@@ -66,15 +66,16 @@ def tile_picked_wema_none_l_kernel(tc, x_words, x_scales, mem, w1, old, new, slo
         nc.sync.dma_start(new_sb[:], new[:, 0:N])
         nc.sync.dma_start(mems[1][:], mem[P : 2 * P, :])
 
-        new_ps = ps.tile([P, P], F32, name="new_ps", tag="bank7")
-        nc.tensor.transpose(new_ps[:], new_rows[:], ident[:])
-        new_col = sb.tile([P, 4], F32, name="new_col")
-        nc.vector.tensor_copy(new_col[:], new_ps[:, P - 4 : P])
         old_ps = ps.tile([P, 4, P], F32, name="old_ps", tag="bank0")
         for b in range(4):
             nc.tensor.transpose(old_ps[:, b, :], old_col[:, b : b + 1].to_broadcast([P, P]), ident[:])
         old_sb = sb.tile([P, T], F32, name="old_sb")
-        nc.scalar.copy(old_sb[:].rearrange("p (n b) -> p n b", b=4), old_ps[:].rearrange("p b n -> p n b"))
+        for h in range(2):
+            nc.scalar.copy(old_sb[:, h * N : (h + 1) * N].rearrange("p (n b) -> p n b", b=4), old_ps[:, :, h * 64 : (h + 1) * 64].rearrange("p b n -> p n b"))
+        new_ps = ps.tile([P, P], F32, name="new_ps", tag="bank7")
+        nc.tensor.transpose(new_ps[:], new_rows[:], ident[:])
+        new_col = sb.tile([P, 4], F32, name="new_col")
+        nc.scalar.copy(new_col[:], new_ps[:, P - 4 : P])
 
         grouped = [sb.tile([P, P, PACK], BF16, name=f"grouped{b}", align_bytes=64) for b in range(2)]
         wq = sb.tile([P, N], U32, name="wq", align_bytes=64)

@@ -97,36 +97,39 @@ def tile_picked_wema_none_l_kernel(tc, x_words, x_scales, mem, w1, old, new, slo
         fetch(0, 0, N)
         fetch(0, N, 3 * P)
 
-        scaled = []
-        for c in range(4):
-            width = P if c < 2 else N
-            yt = ps.tile([P, width], F32, name=f"yt{c}", tag=f"bank{2 + c}")
+        def product(c, lo, hi, bank):
+            yt = ps.tile([P, hi - lo], F32, name=f"yt{c}_{lo}", tag=f"bank{bank}")
             nc.tensor.matmul_mx(out=yt[:], lhsT=xw[:, c * P : (c + 1) * P].bitcast(FP8X4), lhsT_scale=xs[:, c * P : (c + 1) * P],
-                                rhs=wq[:, 0:width].bitcast(FP8X4), rhs_scale=ws[:, 0:width], start=True, stop=True)
-            z = sb.tile([P, width], F32, name=f"z{c}")
+                                rhs=wq[:, lo:hi].bitcast(FP8X4), rhs_scale=ws[:, lo:hi], start=True, stop=True)
+            z = sb.tile([P, hi - lo], F32, name=f"z{c}_{lo}")
             nc.scalar.activation(z[:], yt[:], COPY, scale=new_col[:, c : c + 1])
-            scaled.append(z)
+            return z
+
+        scaled = [product(c, 0, P, 2 + c)[:] for c in range(2)]
+        both = product(2, 0, N, 4)
+        late = [both[:, P:N], product(3, P, N, 5)[:]]
+        scaled.extend([both[:, 0:P], product(3, 0, P, 1)[:]])
         plain = sb.tile([P, P], F32, name="plain")
         nc.scalar.activation(plain[:], mems[0][:].indirect(offs[:, 24:32]), COPY)
 
         def put(lo, hi, bank, total):
             back = ps.tile([P, hi - lo, P], F32, name=f"back{lo}", tag=f"bank{bank}")
             for c in range(lo, hi):
-                nc.tensor.transpose(back[:, c - lo, :], scaled[c][:, 0:P], ident[:])
+                nc.tensor.transpose(back[:, c - lo, :], scaled[c], ident[:])
             nc.vector.tensor_tensor(total, back[:].rearrange("p c n -> p (c n)"), kept[0][:, lo * P : hi * P], ADD)
             nc.scalar.activation(mems[0][:].indirect(offs[:, lo * 8 : hi * 8]), total, COPY)
 
         sums = sb.tile([P, N], F32, name="sums")
         put(0, 2, 7, sums[:])
-        y1 = ps.tile([P, N], F32, name="y1", tag="bank1")
+        y1 = ps.tile([P, N], F32, name="y1", tag="bank0")
         nc.tensor.matmul_mx(out=y1[:], lhsT=wq[:, P:N].bitcast(FP8X4), lhsT_scale=ws[:, P:N], rhs=xw[:, 0:N].bitcast(FP8X4), rhs_scale=xs[:, 0:N], start=True, stop=True)
         nc.vector.tensor_tensor(kept[0][:, 3 * P : T], plain[:], old_sb[:, 3 * P : T], MULT)
         fresh = sb.tile([P, T], F32, name="fresh")
         nc.vector.tensor_tensor(fresh[:, 0:N], y1[:], new_sb[:], MULT)
-        turned_back = ps.tile([P, 2, P], F32, name="turned_back", tag="bank2")
         for c in (2, 3):
-            nc.tensor.transpose(turned_back[:, c - 2, :], scaled[c][:, P:N], ident[:])
-        nc.scalar.copy(fresh[:, N:T], turned_back[:].rearrange("p c n -> p (c n)"))
+            turned_back = ps.tile([P, P], F32, name=f"turned_back{c}", tag=f"bank{c}")
+            nc.tensor.transpose(turned_back[:], late[c - 2], ident[:])
+            nc.scalar.copy(fresh[:, c * P : (c + 1) * P], turned_back[:])
         fetch(1, 0, N)
         fetch(1, N, T)
         put(2, 4, 6, old_sb[:, 0:N])

from contextlib import ExitStack

import concourse.mybir as mybir

K, T, N, U = 512, 512, 256, 1024
FLOPS = 2 * K * T * N
P = 128
PACK = 4

F32 = mybir.dt.float32
BF16 = mybir.dt.bfloat16
I32 = mybir.dt.int32
U32 = mybir.dt.uint32
U16 = mybir.dt.uint16
U8 = mybir.dt.uint8
FP8X4 = mybir.dt.float8_e4m3fn_x4
MULT = mybir.AluOpType.mult
ADD = mybir.AluOpType.add
COPY = mybir.ActivationFunctionType.Copy


def tile_picked_wema_none_l_kernel(tc, x_words, x_scales, mem, w1, old, new, slot, out):
    nc = tc.nc
    with ExitStack() as ctx:
        sb = ctx.enter_context(tc.tile_pool(name="sb", bufs=1))
        ps = ctx.enter_context(tc.psum_pool(name="ps", bufs=1))

        offs = sb.tile([P, T // 16], U16, name="offs")
        w_raw = sb.tile([P, PACK, N], F32, name="w_raw")
        xw = sb.tile([P, T], U32, name="xw", align_bytes=64)
        xs = sb.tile([P, T], U8, name="xs", align_bytes=64)
        old_col = sb.tile([P, 4], F32, name="old_col")
        new_rows = sb.tile([P, P], F32, name="new_rows")
        ident = sb.tile([P, P], F32, name="ident")

        nc.vector.memset(xs[:].bitcast(I32), 0)
        first = sb.tile([P, 1], F32, name="first")
        for q in range(4):
            nc.gpsimd.memset(first[32 * q : 32 * q + 32, :], 32.0 * q)
        nc.gpsimd.memset(new_rows[0:96, :], 0.0)
        nc.gpsimd.memset(new_rows[96 : P - 4, :], 0.0)
        ones = sb.tile([P, P], F32, name="ones")
        ramp = sb.tile([P, P], F32, name="ramp", align_bytes=64)
        turned = sb.tile([P, 32], F32, name="turned", align_bytes=64)
        nc.vector.memset(ones[:], 1.0)
        nc.vector.tensor_tensor_scan(ramp[:], ones[:], ones[:], 0.0, MULT, ADD)
        nc.vector.transpose(turned[:], ramp[:, 0:32])
        nc.vector.tensor_scalar(ident[:], ramp[:], first[:], turned[:, 0:1], mybir.AluOpType.subtract, mybir.AluOpType.is_equal)

        mems = [sb.tile([P, U], F32, name=f"mem{b}") for b in range(2)]
        new_sb = sb.tile([P, N], F32, name="new_sb")
        nc.sync.dma_start(old_col[:], old[0, :].rearrange("(p b) -> p b", b=4))
        nc.scalar.dma_start(new_rows[P - 4 : P, :], new[0, :].rearrange("(c n) -> c n", n=P))
        nc.sync.dma_start(w_raw[:], w1.rearrange("(p j) n -> p j n", j=PACK))

        def load_scales(queue, q):
            queue.dma_start(xs[32 * q : 32 * q + 4, :].bitcast(I32), x_scales[0, 4 * q : 4 * q + 4, :].bitcast(I32))

        load_scales(nc.scalar, 0)
        nc.scalar.dma_start(xw[:].bitcast(I32), x_words[0].rearrange("p n t -> p (n t)").bitcast(I32))
        load_scales(nc.scalar, 1)
        load_scales(nc.sync, 3)
        load_scales(nc.scalar, 2)
        nc.sync.dma_start(mems[0][:], mem[0:P, :])
        nc.sync.dma_start(offs[:], slot)
        nc.sync.dma_start(new_sb[:], new[:, 0:N])
        nc.sync.dma_start(mems[1][:], mem[P : 2 * P, :])

        old_ps = ps.tile([P, 4, P], F32, name="old_ps", tag="bank0")
        for b in range(4):
            nc.tensor.transpose(old_ps[:, b, :], old_col[:, b : b + 1].to_broadcast([P, P]), ident[:])
        old_sb = sb.tile([P, T], F32, name="old_sb")
        for h in range(2):
            nc.scalar.copy(old_sb[:, h * N : (h + 1) * N].rearrange("p (n b) -> p n b", b=4), old_ps[:, :, h * 64 : (h + 1) * 64].rearrange("p b n -> p n b"))
        new_ps = ps.tile([P, P], F32, name="new_ps", tag="bank7")
        nc.tensor.transpose(new_ps[:], new_rows[:], ident[:])
        new_col = sb.tile([P, 4], F32, name="new_col")
        nc.scalar.copy(new_col[:], new_ps[:, P - 4 : P])

        grouped = [sb.tile([P, P, PACK], BF16, name=f"grouped{b}", align_bytes=64) for b in range(2)]
        wq = sb.tile([P, N], U32, name="wq", align_bytes=64)
        ws = sb.tile([P, N], U8, name="ws", align_bytes=64)
        for b in range(2):
            nc.vector.tensor_copy(
                grouped[b][:].rearrange("p (c i) t -> p c t i", i=4),
                w_raw[:, :, b * P : (b + 1) * P].rearrange("p t (c i) -> p c t i", i=4),
            )
        for b in range(2):
            rows = slice(b * P, (b + 1) * P)
            nc.vector.quantize_mx(out=wq[:, rows].bitcast(FP8X4), scales=ws[:, rows], in_=grouped[b][:].rearrange("p n t -> p (n t)"))

        kept = [sb.tile([P, T], F32, name=f"kept{b}") for b in range(2)]

        def fetch(b, lo, hi):
            nc.vector.tensor_tensor(kept[b][:, lo:hi], mems[b][:].indirect(offs[:, lo // 16 : hi // 16]), old_sb[:, lo:hi], MULT)

        fetch(0, 0, N)
        fetch(0, N, 3 * P)

        def product(c, lo, hi, bank):
            yt = ps.tile([P, hi - lo], F32, name=f"yt{c}_{lo}", tag=f"bank{bank}")
            nc.tensor.matmul_mx(out=yt[:], lhsT=xw[:, c * P : (c + 1) * P].bitcast(FP8X4), lhsT_scale=xs[:, c * P : (c + 1) * P],
                                rhs=wq[:, lo:hi].bitcast(FP8X4), rhs_scale=ws[:, lo:hi], start=True, stop=True)
            z = sb.tile([P, hi - lo], F32, name=f"z{c}_{lo}")
            nc.scalar.activation(z[:], yt[:], COPY, scale=new_col[:, c : c + 1])
            return z

        scaled = [product(c, 0, P, 2 + c)[:] for c in range(2)]
        both = product(2, 0, N, 4)
        late = [both[:, P:N], product(3, P, N, 5)[:]]
        scaled.extend([both[:, 0:P], product(3, 0, P, 1)[:]])
        plain = sb.tile([P, P], F32, name="plain")
        nc.scalar.activation(plain[:], mems[0][:].indirect(offs[:, 24:32]), COPY)

        def put(lo, hi, bank, total):
            back = ps.tile([P, hi - lo, P], F32, name=f"back{lo}", tag=f"bank{bank}")
            for c in range(lo, hi):
                nc.tensor.transpose(back[:, c - lo, :], scaled[c], ident[:])
            nc.vector.tensor_tensor(total, back[:].rearrange("p c n -> p (c n)"), kept[0][:, lo * P : hi * P], ADD)
            nc.scalar.activation(mems[0][:].indirect(offs[:, lo * 8 : hi * 8]), total, COPY)

        sums = sb.tile([P, N], F32, name="sums")
        put(0, 2, 7, sums[:])
        y1 = ps.tile([P, N], F32, name="y1", tag="bank0")
        nc.tensor.matmul_mx(out=y1[:], lhsT=wq[:, P:N].bitcast(FP8X4), lhsT_scale=ws[:, P:N], rhs=xw[:, 0:N].bitcast(FP8X4), rhs_scale=xs[:, 0:N], start=True, stop=True)
        nc.vector.tensor_tensor(kept[0][:, 3 * P : T], plain[:], old_sb[:, 3 * P : T], MULT)
        fresh = sb.tile([P, T], F32, name="fresh")
        nc.vector.tensor_tensor(fresh[:, 0:N], y1[:], new_sb[:], MULT)
        for c in (2, 3):
            turned_back = ps.tile([P, P], F32, name=f"turned_back{c}", tag=f"bank{c}")
            nc.tensor.transpose(turned_back[:], late[c - 2], ident[:])
            nc.scalar.copy(fresh[:, c * P : (c + 1) * P], turned_back[:])
        fetch(1, 0, N)
        fetch(1, N, T)
        put(2, 4, 6, old_sb[:, 0:N])
        nc.vector.tensor_tensor(mems[1][:].indirect(offs[:]), kept[1][:], fresh[:], ADD)
        for b in range(2):
            nc.sync.dma_start(out[b * P : (b + 1) * P, :], mems[b][:])
